import numpy as np
import ml_dtypes


def mxq(x, axis, fmt="e4m3"):
    dtype, down = {"e4m3": (ml_dtypes.float8_e4m3fn, 7), "e5m2": (ml_dtypes.float8_e5m2, 14)}[fmt]
    v = np.moveaxis(np.asarray(x, np.float32).astype(ml_dtypes.bfloat16).astype(np.float64), axis, -1)
    blocks = v.reshape(v.shape[:-1] + (-1, 32))
    amax = np.abs(blocks).max(-1, keepdims=True)
    byte = np.maximum(np.where(amax > 0, np.frexp(amax)[1] - 1 + 127, 0) - down, 1)
    scale = np.exp2(byte - 127.0)
    codes = (blocks / scale).astype(np.float32).astype(dtype).astype(np.float64)
    return np.moveaxis((codes * scale).reshape(v.shape), -1, axis)


WIDE = False


def mx_kscale(k):
    if not WIDE:
        return np.ones(k)
    levels = np.array([10, -10, 5, -5, 0])
    if k % 512:
        return np.exp2(np.random.permutation(np.resize(levels, k // 32))).repeat(32)
    a = np.empty((k // 512, 16))
    for p in range(k // 512):
        a[p, :8] = np.random.permutation(np.resize(levels, 8))
        for g in range(8):
            far = levels[np.abs(levels - a[p, g]) >= 10]
            a[p, g + 8] = far[np.random.randint(len(far))]
    return np.exp2(a.ravel()).repeat(32)


def f64(x):
    return np.asarray(x).astype(np.float64)


def striped8(idx):
    return np.asarray(idx).reshape(8, -1, 16).transpose(0, 2, 1).reshape(128, -1).astype(np.uint16)


def unstriped8(offs):
    return offs.reshape(8, 16, -1).transpose(0, 2, 1).reshape(8, -1).astype(np.int64)


def pick8(x, idx, run):
    r = np.arange(len(x))
    return x[r[:, None], idx[r % (8 * run) // run]]


E2M1 = np.array([0.0, 0.5, 1.0, 1.5, 2.0, 3.0, 4.0, 6.0, -0.0, -0.5, -1.0, -1.5, -2.0, -3.0, -4.0, -6.0])


def pack_weight(w, fmt):
    k, n = w.shape
    w = f64(np.asarray(w, np.float32).astype(ml_dtypes.bfloat16)).reshape(k // 32, 32, n)
    amax = np.abs(w).max(1)
    if fmt == "e4m3":
        byte = np.frexp(amax)[1] - 1 + 127 - 7
    else:
        mant, ex = np.frexp(amax / 6.0)
        byte = np.where(mant > 0.5, ex, ex - 1) + 127
    byte = np.clip(np.where(amax > 0, byte, 1), 1, 254)
    scaled = (w * np.exp2(127.0 - byte)[:, None, :]).reshape(k, n).astype(np.float32)
    by_word = np.ascontiguousarray(scaled.reshape(k // 512, 128, 4, n).transpose(0, 1, 3, 2))
    if fmt == "e4m3":
        words = by_word.astype(ml_dtypes.float8_e4m3fn).view(np.uint8)
    else:
        c = by_word.astype(ml_dtypes.float4_e2m1fn).view(np.uint8) & 0xF
        words = (c[..., 0::2] | (c[..., 1::2] << 4)).reshape(k // 512, 128, 2 * n)
    return np.ascontiguousarray(words), np.ascontiguousarray(byte.astype(np.uint8).reshape(k // 512, 16, n))


def unpack_weight(words, scales, fmt):
    g, _, n = scales.shape
    words = np.ascontiguousarray(words).reshape(g, 128, n, -1)
    if fmt == "e4m3":
        vals = words.view(ml_dtypes.float8_e4m3fn).astype(np.float64)
    else:
        nib = np.empty((g, 128, n, 4), np.uint8)
        nib[..., 0::2] = words & 0xF
        nib[..., 1::2] = words >> 4
        vals = E2M1[nib]
    vals = vals * np.repeat(np.exp2(scales.astype(np.float64) - 127.0), 8, axis=1)[..., None]
    return vals.transpose(0, 1, 3, 2).reshape(g * 512, n)


D, T, U, X, S, I, Q = 512, 1024, 1024, 1024, 1024, 512, 128


def setup_inputs():
    n = np.random.standard_normal
    idx = np.stack([np.random.permutation(T)[:I] for _ in range(8)])
    idx2 = np.stack([np.random.permutation(U)[:I] for _ in range(8)])
    idx3 = np.stack([np.random.permutation(X)[:I] for _ in range(8)])
    idx4 = np.stack([np.random.permutation(S)[:I] for _ in range(8)])
    idx5 = np.stack([np.random.permutation(U)[:I] for _ in range(8)])
    idx6 = np.stack([np.random.permutation(S)[:I] for _ in range(8)])
    fd = mx_kscale(D)
    keysp = pack_weight(n((D, T)) / fd[:, None], "e4m3")
    notesp = pack_weight(n((D, U)) / fd[:, None], "e2m1")
    usersp = pack_weight(n((D, X)) / fd[:, None], "e4m3")
    shelvesp = pack_weight(n((D, S)) / fd[:, None], "e2m1")
    return {
        "query": (n((D, Q)) * 1.0 / np.sqrt(D) * fd[:, None]).astype(np.float32),
        "keys_words": keysp[0],
        "keys_scales": keysp[1],
        "notes_words": notesp[0],
        "notes_scales": notesp[1],
        "users_words": usersp[0],
        "users_scales": usersp[1],
        "shelves_words": shelvesp[0],
        "shelves_scales": shelvesp[1],
        "offs": striped8(idx),
        "offs2": striped8(idx2),
        "offs3": striped8(idx3),
        "offs4": striped8(idx4),
        "offs5": striped8(idx5),
        "offs6": striped8(idx6),
    }


def reference(query, keys_words, keys_scales, notes_words, notes_scales, users_words, users_scales, shelves_words, shelves_scales, offs, offs2, offs3, offs4, offs5, offs6):
    idx = unstriped8(offs)
    idx2 = unstriped8(offs2)
    idx3 = unstriped8(offs3)
    idx4 = unstriped8(offs4)
    idx5 = unstriped8(offs5)
    idx6 = unstriped8(offs6)
    keysu = unpack_weight(keys_words, keys_scales, "e4m3")
    notesu = unpack_weight(notes_words, notes_scales, "e2m1")
    usersu = unpack_weight(users_words, users_scales, "e4m3")
    shelvesu = unpack_weight(shelves_words, shelves_scales, "e2m1")
    queryq = mxq(f64(query), 0, "e4m3")
    a = queryq.T @ keysu
    b = queryq.T @ notesu
    c0 = queryq.T @ usersu
    d0 = queryq.T @ shelvesu
    f1 = np.zeros((Q, U))
    f1[np.arange(Q)[:, None], idx2[np.arange(Q) % 128 // 16]] = pick8(a, idx, 16)
    f2 = np.zeros((Q, S))
    f2[np.arange(Q)[:, None], idx4[np.arange(Q) % 128 // 16]] = pick8(c0, idx3, 16)
    bb = b + f1
    dd = d0 - f2
    y = np.maximum(pick8(bb, idx5, 16), pick8(dd, idx6, 16))
    return y

@@ -1,0 +1,168 @@
+from contextlib import ExitStack
+
+import concourse.mybir as mybir
+
+D, COLS, SLOTS, Q = 512, 1024, 512, 128
+FLOPS = 2 * D * Q * 4 * COLS
+
+F32 = mybir.dt.float32
+BF16 = mybir.dt.bfloat16
+I32 = mybir.dt.int32
+U32 = mybir.dt.uint32
+U16 = mybir.dt.uint16
+U8 = mybir.dt.uint8
+FP8X4 = mybir.dt.float8_e4m3fn_x4
+FP4X4 = mybir.dt.float4_e2m1fn_x4
+COPY = mybir.ActivationFunctionType.Copy
+ALU = mybir.AluOpType
+
+P = 128
+PACK = 4
+BANK = 512
+HALF_SLOTS = SLOTS // 2
+LIST_COLS = SLOTS // 16
+HALF_LIST = LIST_COLS // 2
+CAST_V = 80
+
+
+def tile_attend_twomarkets_four_kernel(
+    tc, query, keys_words, keys_scales, notes_words, notes_scales, users_words, users_scales,
+    shelves_words, shelves_scales, offs, offs2, offs3, offs4, offs5, offs6, out,
+):
+    nc = tc.nc
+    with ExitStack() as ctx:
+        lists = ctx.enter_context(tc.tile_pool(name="lists", bufs=1))
+        sb = ctx.enter_context(tc.tile_pool(name="sb", bufs=1))
+        psum = ctx.enter_context(tc.psum_pool(name="psum", bufs=1))
+
+        def load_list(source, name):
+            tile = lists.tile([P, LIST_COLS], U16, name=name)
+            nc.sync.dma_start(tile[:], source)
+            return tile
+
+        def zeroed_plane(name):
+            plane = sb.tile([P, COLS], U8, name=name, align_bytes=64)
+            nc.vector.memset(plane[:].bitcast(I32), 0)
+            return plane
+
+        def load_scales(plane, scales):
+            for quad in range(4):
+                nc.sync.dma_start(
+                    plane[32 * quad : 32 * quad + 4, :].bitcast(I32),
+                    scales[0, 4 * quad : 4 * quad + 4, :].bitcast(I32),
+                )
+
+        def load_fp8_words(words, name, tag):
+            tile = sb.tile([P, COLS], U32, name=name, tag=tag, align_bytes=64)
+            nc.sync.dma_start(tile[:].bitcast(I32), words[0].rearrange("p n t -> p (n t)").bitcast(I32))
+            return tile
+
+        def load_fp4_words(words, name):
+            tile = sb.tile([P, 2 * COLS], U8, name=name, align_bytes=64)
+            nc.sync.dma_start(tile[:].bitcast(I32), words[0].bitcast(I32))
+            return tile
+
+        keys_plane = zeroed_plane("keys_plane")
+        q_raw = sb.tile([P, PACK, Q], F32, name="q_raw", align_bytes=64)
+        nc.sync.dma_start(q_raw[:], query.rearrange("(p j) w -> p j w", j=PACK))
+        keys_w = load_fp8_words(keys_words, "keys_w", "keys_w")
+        load_scales(keys_plane, keys_scales)
+        idx = load_list(offs, "idx")
+        idx2 = load_list(offs2, "idx2")
+
+        users_plane = zeroed_plane("users_plane")
+        notes_plane = zeroed_plane("notes_plane")
+        shelves_plane = zeroed_plane("shelves_plane")
+        f1 = sb.tile([P, COLS], F32, name="f1")
+        nc.vector.memset(f1[:], 0.0)
+
+        q_bf = sb.tile([P, Q, PACK], BF16, name="q_bf", tag="q_bf_then_f2", align_bytes=64)
+        nc.vector.tensor_copy(
+            out=q_bf[:, :CAST_V, :].rearrange("p (c i) t -> p c t i", i=4),
+            in_=q_raw[:, :, :CAST_V].rearrange("p t (c i) -> p c t i", i=4),
+        )
+        nc.scalar.copy(
+            out=q_bf[:, CAST_V:, :].rearrange("p (c i) t -> p c t i", i=4),
+            in_=q_raw[:, :, CAST_V:].rearrange("p t (c i) -> p c t i", i=4),
+        )
+        q_codes = sb.tile([P, Q], U32, name="q_codes", align_bytes=64)
+        q_plane = sb.tile([P, Q], U8, name="q_plane", align_bytes=64)
+        nc.vector.quantize_mx(
+            out=q_codes[:].bitcast(FP8X4), scales=q_plane[:], in_=q_bf[:].rearrange("p w t -> p (w t)")
+        )
+        f2 = sb.tile([P, COLS], F32, name="f2", tag="q_bf_then_f2", align_bytes=64)
+        nc.vector.memset(f2[:], 0.0)
+
+        users_w = load_fp8_words(users_words, "users_w", "users_w")
+        load_scales(users_plane, users_scales)
+        idx3 = load_list(offs3, "idx3")
+        idx4 = load_list(offs4, "idx4")
+        notes_w = load_fp4_words(notes_words, "notes_w")
+        load_scales(notes_plane, notes_scales)
+        idx5 = load_list(offs5, "idx5")
+        shelves_w = load_fp4_words(shelves_words, "shelves_w")
+        load_scales(shelves_plane, shelves_scales)
+        idx6 = load_list(offs6, "idx6")
+
+        def score(moving, plane, c0, width, bank):
+            acc = psum.tile([P, width], F32, name="acc", tag="bank%d" % bank)
+            nc.tensor.matmul_mx(
+                out=acc[:], lhsT=q_codes[:].bitcast(FP8X4), lhsT_scale=q_plane[:],
+                rhs=moving, rhs_scale=plane[:, c0 : c0 + width], start=True, stop=True,
+            )
+            return acc
+
+        def fp8_cols(tile, c0, width):
+            return tile[:, c0 : c0 + width].bitcast(FP8X4)
+
+        def fp4_cols(tile, c0, width):
+            return tile[:, 2 * c0 : 2 * (c0 + width)].bitcast(FP4X4)
+
+        a_sb = sb.tile([P, COLS], F32, name="a_sb")
+        for j in range(4):
+            c0 = 256 * j
+            acc = score(fp8_cols(keys_w, c0, 256), keys_plane, c0, 256, j)
+            if j % 2 == 0:
+                nc.scalar.copy(a_sb[:, c0 : c0 + 256], acc[:])
+            else:
+                nc.vector.tensor_copy(a_sb[:, c0 : c0 + 256], acc[:])
+        a_lo = sb.tile([P, HALF_SLOTS], F32, name="a_lo")
+        a_hi = sb.tile([P, HALF_SLOTS], F32, name="a_hi")
+        nc.vector.tensor_copy(a_lo[:], a_sb[:].indirect(idx[:, :HALF_LIST]))
+        nc.scalar.activation(a_hi[:], a_sb[:].indirect(idx[:, HALF_LIST:]), COPY)
+        nc.vector.tensor_copy(f1[:].indirect(idx2[:, :HALF_LIST]), a_lo[:])
+        nc.vector.tensor_copy(f1[:].indirect(idx2[:, HALF_LIST:]), a_hi[:])
+
+        c_sb = sb.tile([P, COLS], F32, name="c_sb")
+        for j in range(2):
+            c0 = BANK * j
+            acc = score(fp8_cols(users_w, c0, BANK), users_plane, c0, BANK, 4 + j)
+            nc.scalar.copy(c_sb[:, c0 : c0 + BANK], acc[:])
+        c_pick = sb.tile([P, SLOTS], F32, name="c_pick")
+        nc.scalar.activation(c_pick[:], c_sb[:].indirect(idx3[:]), COPY)
+        nc.vector.tensor_copy(f2[:].indirect(idx4[:]), c_pick[:])
+
+        b_sb = sb.tile([P, COLS], F32, name="b_sb")
+        bb = sb.tile([P, COLS], F32, name="bb")
+        for j in range(2):
+            c0 = BANK * j
+            acc = score(fp4_cols(notes_w, c0, BANK), notes_plane, c0, BANK, 6 + j)
+            nc.scalar.copy(b_sb[:, c0 : c0 + BANK], acc[:])
+            nc.gpsimd.tensor_tensor(bb[:, c0 : c0 + BANK], b_sb[:, c0 : c0 + BANK], f1[:, c0 : c0 + BANK], ALU.add)
+        bb_pick = sb.tile([P, SLOTS], F32, name="bb_pick")
+        nc.scalar.activation(bb_pick[:], bb[:].indirect(idx5[:]), COPY)
+
+        dd = sb.tile([P, COLS], F32, name="dd")
+        for j in range(2):
+            c0 = BANK * j
+            acc = score(fp4_cols(shelves_w, c0, BANK), shelves_plane, c0, BANK, j)
+            nc.vector.tensor_tensor(dd[:, c0 : c0 + BANK], acc[:], f2[:, c0 : c0 + BANK], ALU.subtract)
+        dd_lo = sb.tile([P, HALF_SLOTS], F32, name="dd_lo")
+        dd_hi = sb.tile([P, HALF_SLOTS], F32, name="dd_hi")
+        nc.vector.tensor_copy(dd_lo[:], dd[:].indirect(idx6[:, :HALF_LIST]))
+        nc.scalar.activation(dd_hi[:], dd[:].indirect(idx6[:, HALF_LIST:]), COPY)
+        for j, picked in enumerate((dd_lo, dd_hi)):
+            cols = slice(j * HALF_SLOTS, (j + 1) * HALF_SLOTS)
+            y = sb.tile([P, HALF_SLOTS], F32, name="y%d" % j)
+            nc.vector.tensor_tensor(y[:], picked[:], bb_pick[:, cols], ALU.max)
+            nc.sync.dma_start(out[:, cols], y[:])

@@ -23,6 +23,8 @@ HALF_SLOTS = SLOTS // 2
 LIST_COLS = SLOTS // 16
 HALF_LIST = LIST_COLS // 2
 CAST_V = 80
+SPLIT = 768
+REST = COLS - SPLIT
 
 
 def tile_attend_twomarkets_four_kernel(
@@ -65,10 +67,13 @@ def tile_attend_twomarkets_four_kernel(
         keys_plane = zeroed_plane("keys_plane")
         q_raw = sb.tile([P, PACK, Q], F32, name="q_raw", align_bytes=64)
         nc.sync.dma_start(q_raw[:], query.rearrange("(p j) w -> p j w", j=PACK))
-        keys_w = load_fp8_words(keys_words, "keys_w", "keys_w")
+        keys_rows = keys_words[0].rearrange("p n t -> p (n t)").bitcast(I32)
+        keys_lo = sb.tile([P, BANK], U32, name="keys_lo", align_bytes=64)
+        nc.sync.dma_start(keys_lo[:].bitcast(I32), keys_rows[:, :BANK])
         load_scales(keys_plane, keys_scales)
+        keys_hi = sb.tile([P, BANK], U32, name="keys_hi", align_bytes=64)
+        nc.sync.dma_start(keys_hi[:].bitcast(I32), keys_rows[:, BANK:])
         idx = load_list(offs, "idx")
-        idx2 = load_list(offs2, "idx2")
 
         users_plane = zeroed_plane("users_plane")
         notes_plane = zeroed_plane("notes_plane")
@@ -95,21 +100,28 @@ def tile_attend_twomarkets_four_kernel(
 
         users_w = load_fp8_words(users_words, "users_w", "users_w")
         load_scales(users_plane, users_scales)
+        idx2 = load_list(offs2, "idx2")
         idx3 = load_list(offs3, "idx3")
         idx4 = load_list(offs4, "idx4")
         notes_w = load_fp4_words(notes_words, "notes_w")
         load_scales(notes_plane, notes_scales)
-        idx5 = load_list(offs5, "idx5")
         shelves_w = load_fp4_words(shelves_words, "shelves_w")
         load_scales(shelves_plane, shelves_scales)
+        idx5 = load_list(offs5, "idx5")
         idx6 = load_list(offs6, "idx6")
 
-        def score(moving, plane, c0, width, bank):
-            acc = psum.tile([P, width], F32, name="acc", tag="bank%d" % bank)
+        def bank_tile(bank, width):
+            return psum.tile([P, width], F32, name="acc", tag="bank%d" % bank)
+
+        def score_into(acc, moving, plane, c0, width):
             nc.tensor.matmul_mx(
-                out=acc[:], lhsT=q_codes[:].bitcast(FP8X4), lhsT_scale=q_plane[:],
+                out=acc, lhsT=q_codes[:].bitcast(FP8X4), lhsT_scale=q_plane[:],
                 rhs=moving, rhs_scale=plane[:, c0 : c0 + width], start=True, stop=True,
             )
+
+        def score(moving, plane, c0, width, bank):
+            acc = bank_tile(bank, width)
+            score_into(acc[:], moving, plane, c0, width)
             return acc
 
         def fp8_cols(tile, c0, width):
@@ -121,17 +133,15 @@ def tile_attend_twomarkets_four_kernel(
         a_sb = sb.tile([P, COLS], F32, name="a_sb")
         for j in range(4):
             c0 = 256 * j
-            acc = score(fp8_cols(keys_w, c0, 256), keys_plane, c0, 256, j)
-            if j % 2 == 0:
+            acc = score(fp8_cols((keys_lo, keys_hi)[j // 2], c0 % BANK, 256), keys_plane, c0, 256, j)
+            if j % 2 == 1:
                 nc.scalar.copy(a_sb[:, c0 : c0 + 256], acc[:])
             else:
                 nc.vector.tensor_copy(a_sb[:, c0 : c0 + 256], acc[:])
-        a_lo = sb.tile([P, HALF_SLOTS], F32, name="a_lo")
-        a_hi = sb.tile([P, HALF_SLOTS], F32, name="a_hi")
-        nc.vector.tensor_copy(a_lo[:], a_sb[:].indirect(idx[:, :HALF_LIST]))
-        nc.scalar.activation(a_hi[:], a_sb[:].indirect(idx[:, HALF_LIST:]), COPY)
-        nc.vector.tensor_copy(f1[:].indirect(idx2[:, :HALF_LIST]), a_lo[:])
-        nc.vector.tensor_copy(f1[:].indirect(idx2[:, HALF_LIST:]), a_hi[:])
+        a_pick = sb.tile([P, SLOTS], F32, name="a_pick")
+        nc.vector.tensor_copy(a_pick[:, :HALF_SLOTS], a_sb[:].indirect(idx[:, :HALF_LIST]))
+        nc.scalar.activation(a_pick[:, HALF_SLOTS:], a_sb[:].indirect(idx[:, HALF_LIST:]), COPY)
+        nc.vector.tensor_copy(f1[:].indirect(idx2[:]), a_pick[:])
 
         c_sb = sb.tile([P, COLS], F32, name="c_sb")
         for j in range(2):
@@ -142,26 +152,31 @@ def tile_attend_twomarkets_four_kernel(
         nc.scalar.activation(c_pick[:], c_sb[:].indirect(idx3[:]), COPY)
         nc.vector.tensor_copy(f2[:].indirect(idx4[:]), c_pick[:])
 
-        b_sb = sb.tile([P, COLS], F32, name="b_sb")
+        b_sb = sb.tile([P, SPLIT], F32, name="b_sb")
         bb = sb.tile([P, COLS], F32, name="bb")
-        for j in range(2):
-            c0 = BANK * j
-            acc = score(fp4_cols(notes_w, c0, BANK), notes_plane, c0, BANK, 6 + j)
-            nc.scalar.copy(b_sb[:, c0 : c0 + BANK], acc[:])
-            nc.gpsimd.tensor_tensor(bb[:, c0 : c0 + BANK], b_sb[:, c0 : c0 + BANK], f1[:, c0 : c0 + BANK], ALU.add)
+        for c0, width, bank in ((0, BANK, 6), (BANK, SPLIT - BANK, 7)):
+            acc = score(fp4_cols(notes_w, c0, width), notes_plane, c0, width, bank)
+            nc.scalar.copy(b_sb[:, c0 : c0 + width], acc[:])
+            nc.gpsimd.tensor_tensor(bb[:, c0 : c0 + width], b_sb[:, c0 : c0 + width], f1[:, c0 : c0 + width], ALU.add)
+        ends = bank_tile(2, 2 * REST)
+        score_into(ends[:, :REST], fp4_cols(notes_w, SPLIT, REST), notes_plane, SPLIT, REST)
+        score_into(ends[:, REST:], fp4_cols(shelves_w, SPLIT, REST), shelves_plane, SPLIT, REST)
+        ends_sb = sb.tile([P, 2 * REST], F32, name="ends_sb")
+        nc.scalar.copy(ends_sb[:], ends[:])
+        nc.gpsimd.tensor_tensor(bb[:, SPLIT:], ends_sb[:, :REST], f1[:, SPLIT:], ALU.add)
         bb_pick = sb.tile([P, SLOTS], F32, name="bb_pick")
         nc.scalar.activation(bb_pick[:], bb[:].indirect(idx5[:]), COPY)
 
         dd = sb.tile([P, COLS], F32, name="dd")
-        for j in range(2):
-            c0 = BANK * j
-            acc = score(fp4_cols(shelves_w, c0, BANK), shelves_plane, c0, BANK, j)
-            nc.vector.tensor_tensor(dd[:, c0 : c0 + BANK], acc[:], f2[:, c0 : c0 + BANK], ALU.subtract)
+        nc.gpsimd.tensor_tensor(dd[:, SPLIT:], ends_sb[:, REST:], f2[:, SPLIT:], ALU.subtract)
+        for c0, width, bank in ((0, BANK, 0), (BANK, SPLIT - BANK, 1)):
+            acc = score(fp4_cols(shelves_w, c0, width), shelves_plane, c0, width, bank)
+            nc.vector.tensor_tensor(dd[:, c0 : c0 + width], acc[:], f2[:, c0 : c0 + width], ALU.subtract)
         dd_lo = sb.tile([P, HALF_SLOTS], F32, name="dd_lo")
         dd_hi = sb.tile([P, HALF_SLOTS], F32, name="dd_hi")
         nc.vector.tensor_copy(dd_lo[:], dd[:].indirect(idx6[:, :HALF_LIST]))
         nc.scalar.activation(dd_hi[:], dd[:].indirect(idx6[:, HALF_LIST:]), COPY)
-        for j, picked in enumerate((dd_lo, dd_hi)):
+        for j, picked in ((1, dd_hi), (0, dd_lo)):
             cols = slice(j * HALF_SLOTS, (j + 1) * HALF_SLOTS)
             y = sb.tile([P, HALF_SLOTS], F32, name="y%d" % j)
             nc.vector.tensor_tensor(y[:], picked[:], bb_pick[:, cols], ALU.max)

@@ -48,7 +48,7 @@ def tile_attend_twomarkets_four_kernel(
             return plane
 
         def load_scales(plane, scales):
-            for quad in range(4):
+            for quad in (0, 2, 1, 3):
                 nc.sync.dma_start(
                     plane[32 * quad : 32 * quad + 4, :].bitcast(I32),
                     scales[0, 4 * quad : 4 * quad + 4, :].bitcast(I32),
@@ -131,13 +131,14 @@ def tile_attend_twomarkets_four_kernel(
             return tile[:, 2 * c0 : 2 * (c0 + width)].bitcast(FP4X4)
 
         a_sb = sb.tile([P, COLS], F32, name="a_sb")
-        for j in range(4):
-            c0 = 256 * j
-            acc = score(fp8_cols((keys_lo, keys_hi)[j // 2], c0 % BANK, 256), keys_plane, c0, 256, j)
-            if j % 2 == 1:
-                nc.scalar.copy(a_sb[:, c0 : c0 + 256], acc[:])
+        c0 = 0
+        for j, width in enumerate((256, 256, 256, 128, 128)):
+            acc = score(fp8_cols((keys_lo, keys_hi)[c0 // BANK], c0 % BANK, width), keys_plane, c0, width, j)
+            if j in (0, 2):
+                nc.vector.tensor_copy(a_sb[:, c0 : c0 + width], acc[:])
             else:
-                nc.vector.tensor_copy(a_sb[:, c0 : c0 + 256], acc[:])
+                nc.scalar.copy(a_sb[:, c0 : c0 + width], acc[:])
+            c0 += width
         a_pick = sb.tile([P, SLOTS], F32, name="a_pick")
         nc.vector.tensor_copy(a_pick[:, :HALF_SLOTS], a_sb[:].indirect(idx[:, :HALF_LIST]))
         nc.scalar.activation(a_pick[:, HALF_SLOTS:], a_sb[:].indirect(idx[:, HALF_LIST:]), COPY)
@@ -146,7 +147,7 @@ def tile_attend_twomarkets_four_kernel(
         c_sb = sb.tile([P, COLS], F32, name="c_sb")
         for j in range(2):
             c0 = BANK * j
-            acc = score(fp8_cols(users_w, c0, BANK), users_plane, c0, BANK, 4 + j)
+            acc = score(fp8_cols(users_w, c0, BANK), users_plane, c0, BANK, 5 + j)
             nc.scalar.copy(c_sb[:, c0 : c0 + BANK], acc[:])
         c_pick = sb.tile([P, SLOTS], F32, name="c_pick")
         nc.scalar.activation(c_pick[:], c_sb[:].indirect(idx3[:]), COPY)
@@ -154,7 +155,7 @@ def tile_attend_twomarkets_four_kernel(
 
         b_sb = sb.tile([P, SPLIT], F32, name="b_sb")
         bb = sb.tile([P, COLS], F32, name="bb")
-        for c0, width, bank in ((0, BANK, 6), (BANK, SPLIT - BANK, 7)):
+        for c0, width, bank in ((0, BANK, 7), (BANK, SPLIT - BANK, 3)):
             acc = score(fp4_cols(notes_w, c0, width), notes_plane, c0, width, bank)
             nc.scalar.copy(b_sb[:, c0 : c0 + width], acc[:])
             nc.gpsimd.tensor_tensor(bb[:, c0 : c0 + width], b_sb[:, c0 : c0 + width], f1[:, c0 : c0 + width], ALU.add)

@@ -2,8 +2,8 @@ from contextlib import ExitStack
 
 import concourse.mybir as mybir
 
-D, COLS, SLOTS, Q = 512, 1024, 512, 128
-FLOPS = 2 * D * Q * 4 * COLS
+FEATURES, COLS, SLOTS, ROWS = 512, 1024, 512, 128
+FLOPS = 2 * FEATURES * ROWS * 4 * COLS
 
 F32 = mybir.dt.float32
 BF16 = mybir.dt.bfloat16
@@ -22,9 +22,13 @@ BANK = 512
 HALF_SLOTS = SLOTS // 2
 LIST_COLS = SLOTS // 16
 HALF_LIST = LIST_COLS // 2
-CAST_V = 80
-SPLIT = 768
-REST = COLS - SPLIT
+
+CAST_ON_VECTOR = 80
+A_WIDTHS = (256, 256, 256, 128, 128)
+A_ON_VECTOR = (0, 2)
+D_SPLIT = 640
+B_REST = BANK - (COLS - D_SPLIT)
+B_SPLIT = COLS - B_REST
 
 
 def tile_attend_twomarkets_four_kernel(
@@ -54,9 +58,10 @@ def tile_attend_twomarkets_four_kernel(
                     scales[0, 4 * quad : 4 * quad + 4, :].bitcast(I32),
                 )
 
-        def load_fp8_words(words, name, tag):
-            tile = sb.tile([P, COLS], U32, name=name, tag=tag, align_bytes=64)
-            nc.sync.dma_start(tile[:].bitcast(I32), words[0].rearrange("p n t -> p (n t)").bitcast(I32))
+        def load_fp8_words(words, first, width, name):
+            tile = sb.tile([P, width], U32, name=name, align_bytes=64)
+            rows = words[0].rearrange("p n t -> p (n t)").bitcast(I32)
+            nc.sync.dma_start(tile[:].bitcast(I32), rows[:, first : first + width])
             return tile
 
         def load_fp4_words(words, name):
@@ -65,14 +70,11 @@ def tile_attend_twomarkets_four_kernel(
             return tile
 
         keys_plane = zeroed_plane("keys_plane")
-        q_raw = sb.tile([P, PACK, Q], F32, name="q_raw", align_bytes=64)
-        nc.sync.dma_start(q_raw[:], query.rearrange("(p j) w -> p j w", j=PACK))
-        keys_rows = keys_words[0].rearrange("p n t -> p (n t)").bitcast(I32)
-        keys_lo = sb.tile([P, BANK], U32, name="keys_lo", align_bytes=64)
-        nc.sync.dma_start(keys_lo[:].bitcast(I32), keys_rows[:, :BANK])
+        q_raw = sb.tile([P, PACK, ROWS], F32, name="q_raw", align_bytes=64)
+        nc.sync.dma_start(q_raw[:], query.rearrange("(p t) w -> p t w", t=PACK))
+        keys_lo = load_fp8_words(keys_words, 0, BANK, "keys_lo")
         load_scales(keys_plane, keys_scales)
-        keys_hi = sb.tile([P, BANK], U32, name="keys_hi", align_bytes=64)
-        nc.sync.dma_start(keys_hi[:].bitcast(I32), keys_rows[:, BANK:])
+        keys_hi = load_fp8_words(keys_words, BANK, BANK, "keys_hi")
         idx = load_list(offs, "idx")
 
         users_plane = zeroed_plane("users_plane")
@@ -81,24 +83,24 @@ def tile_attend_twomarkets_four_kernel(
         f1 = sb.tile([P, COLS], F32, name="f1")
         nc.vector.memset(f1[:], 0.0)
 
-        q_bf = sb.tile([P, Q, PACK], BF16, name="q_bf", tag="q_bf_then_f2", align_bytes=64)
+        q_bf = sb.tile([P, ROWS, PACK], BF16, name="q_bf", tag="q_bf_then_f2", align_bytes=64)
         nc.vector.tensor_copy(
-            out=q_bf[:, :CAST_V, :].rearrange("p (c i) t -> p c t i", i=4),
-            in_=q_raw[:, :, :CAST_V].rearrange("p t (c i) -> p c t i", i=4),
+            out=q_bf[:, :CAST_ON_VECTOR, :].rearrange("p (c i) t -> p c t i", i=4),
+            in_=q_raw[:, :, :CAST_ON_VECTOR].rearrange("p t (c i) -> p c t i", i=4),
         )
         nc.scalar.copy(
-            out=q_bf[:, CAST_V:, :].rearrange("p (c i) t -> p c t i", i=4),
-            in_=q_raw[:, :, CAST_V:].rearrange("p t (c i) -> p c t i", i=4),
+            out=q_bf[:, CAST_ON_VECTOR:, :].rearrange("p (c i) t -> p c t i", i=4),
+            in_=q_raw[:, :, CAST_ON_VECTOR:].rearrange("p t (c i) -> p c t i", i=4),
         )
-        q_codes = sb.tile([P, Q], U32, name="q_codes", align_bytes=64)
-        q_plane = sb.tile([P, Q], U8, name="q_plane", align_bytes=64)
+        q_codes = sb.tile([P, ROWS], U32, name="q_codes", align_bytes=64)
+        q_plane = sb.tile([P, ROWS], U8, name="q_plane", align_bytes=64)
         nc.vector.quantize_mx(
             out=q_codes[:].bitcast(FP8X4), scales=q_plane[:], in_=q_bf[:].rearrange("p w t -> p (w t)")
         )
         f2 = sb.tile([P, COLS], F32, name="f2", tag="q_bf_then_f2", align_bytes=64)
         nc.vector.memset(f2[:], 0.0)
 
-        users_w = load_fp8_words(users_words, "users_w", "users_w")
+        users_w = load_fp8_words(users_words, 0, COLS, "users_w")
         load_scales(users_plane, users_scales)
         idx2 = load_list(offs2, "idx2")
         idx3 = load_list(offs3, "idx3")
@@ -113,72 +115,77 @@ def tile_attend_twomarkets_four_kernel(
         def bank_tile(bank, width):
             return psum.tile([P, width], F32, name="acc", tag="bank%d" % bank)
 
-        def score_into(acc, moving, plane, c0, width):
+        def score(acc, moving, moving_scale):
             nc.tensor.matmul_mx(
                 out=acc, lhsT=q_codes[:].bitcast(FP8X4), lhsT_scale=q_plane[:],
-                rhs=moving, rhs_scale=plane[:, c0 : c0 + width], start=True, stop=True,
+                rhs=moving, rhs_scale=moving_scale, start=True, stop=True,
             )
 
-        def score(moving, plane, c0, width, bank):
-            acc = bank_tile(bank, width)
-            score_into(acc[:], moving, plane, c0, width)
-            return acc
-
-        def fp8_cols(tile, c0, width):
-            return tile[:, c0 : c0 + width].bitcast(FP8X4)
-
-        def fp4_cols(tile, c0, width):
-            return tile[:, 2 * c0 : 2 * (c0 + width)].bitcast(FP4X4)
+        def score_fp4(acc, at, words, plane, first, widths):
+            for width in widths:
+                moving = words[:, 2 * first : 2 * (first + width)].bitcast(FP4X4)
+                score(acc[:, at : at + width], moving, plane[:, first : first + width])
+                at += width
+                first += width
 
         a_sb = sb.tile([P, COLS], F32, name="a_sb")
-        c0 = 0
-        for j, width in enumerate((256, 256, 256, 128, 128)):
-            acc = score(fp8_cols((keys_lo, keys_hi)[c0 // BANK], c0 % BANK, width), keys_plane, c0, width, j)
-            if j in (0, 2):
-                nc.vector.tensor_copy(a_sb[:, c0 : c0 + width], acc[:])
+        first = 0
+        for piece, width in enumerate(A_WIDTHS):
+            cols = slice(first, first + width)
+            keys_half = (keys_lo, keys_hi)[first // BANK]
+            acc = bank_tile(piece, width)
+            score(acc[:], keys_half[:, first % BANK : first % BANK + width].bitcast(FP8X4), keys_plane[:, cols])
+            if piece in A_ON_VECTOR:
+                nc.vector.tensor_copy(a_sb[:, cols], acc[:])
             else:
-                nc.scalar.copy(a_sb[:, c0 : c0 + width], acc[:])
-            c0 += width
+                nc.scalar.copy(a_sb[:, cols], acc[:])
+            first += width
         a_pick = sb.tile([P, SLOTS], F32, name="a_pick")
         nc.vector.tensor_copy(a_pick[:, :HALF_SLOTS], a_sb[:].indirect(idx[:, :HALF_LIST]))
         nc.scalar.activation(a_pick[:, HALF_SLOTS:], a_sb[:].indirect(idx[:, HALF_LIST:]), COPY)
         nc.vector.tensor_copy(f1[:].indirect(idx2[:]), a_pick[:])
 
         c_sb = sb.tile([P, COLS], F32, name="c_sb")
-        for j in range(2):
-            c0 = BANK * j
-            acc = score(fp8_cols(users_w, c0, BANK), users_plane, c0, BANK, 5 + j)
-            nc.scalar.copy(c_sb[:, c0 : c0 + BANK], acc[:])
+        for half in range(2):
+            cols = slice(half * BANK, (half + 1) * BANK)
+            acc = bank_tile(5 + half, BANK)
+            score(acc[:], users_w[:, cols].bitcast(FP8X4), users_plane[:, cols])
+            nc.scalar.copy(c_sb[:, cols], acc[:])
         c_pick = sb.tile([P, SLOTS], F32, name="c_pick")
         nc.scalar.activation(c_pick[:], c_sb[:].indirect(idx3[:]), COPY)
         nc.vector.tensor_copy(f2[:].indirect(idx4[:]), c_pick[:])
 
-        b_sb = sb.tile([P, SPLIT], F32, name="b_sb")
+        b_sb = sb.tile([P, B_SPLIT], F32, name="b_sb")
         bb = sb.tile([P, COLS], F32, name="bb")
-        for c0, width, bank in ((0, BANK, 7), (BANK, SPLIT - BANK, 3)):
-            acc = score(fp4_cols(notes_w, c0, width), notes_plane, c0, width, bank)
-            nc.scalar.copy(b_sb[:, c0 : c0 + width], acc[:])
-            nc.gpsimd.tensor_tensor(bb[:, c0 : c0 + width], b_sb[:, c0 : c0 + width], f1[:, c0 : c0 + width], ALU.add)
-        ends = bank_tile(2, 2 * REST)
-        score_into(ends[:, :REST], fp4_cols(notes_w, SPLIT, REST), notes_plane, SPLIT, REST)
-        score_into(ends[:, REST:], fp4_cols(shelves_w, SPLIT, REST), shelves_plane, SPLIT, REST)
-        ends_sb = sb.tile([P, 2 * REST], F32, name="ends_sb")
+        for first, widths, bank in ((0, (BANK,), 7), (BANK, (256, 128), 3)):
+            cols = slice(first, first + sum(widths))
+            acc = bank_tile(bank, sum(widths))
+            score_fp4(acc, 0, notes_w, notes_plane, first, widths)
+            nc.scalar.copy(b_sb[:, cols], acc[:])
+            nc.gpsimd.tensor_tensor(bb[:, cols], b_sb[:, cols], f1[:, cols], ALU.add)
+        ends = bank_tile(2, BANK)
+        score_fp4(ends, 0, notes_w, notes_plane, B_SPLIT, (B_REST,))
+        score_fp4(ends, B_REST, shelves_w, shelves_plane, D_SPLIT, (256, 128))
+        ends_sb = sb.tile([P, BANK], F32, name="ends_sb")
         nc.scalar.copy(ends_sb[:], ends[:])
-        nc.gpsimd.tensor_tensor(bb[:, SPLIT:], ends_sb[:, :REST], f1[:, SPLIT:], ALU.add)
+        nc.gpsimd.tensor_tensor(bb[:, B_SPLIT:], ends_sb[:, :B_REST], f1[:, B_SPLIT:], ALU.add)
         bb_pick = sb.tile([P, SLOTS], F32, name="bb_pick")
         nc.scalar.activation(bb_pick[:], bb[:].indirect(idx5[:]), COPY)
 
         dd = sb.tile([P, COLS], F32, name="dd")
-        nc.gpsimd.tensor_tensor(dd[:, SPLIT:], ends_sb[:, REST:], f2[:, SPLIT:], ALU.subtract)
-        for c0, width, bank in ((0, BANK, 0), (BANK, SPLIT - BANK, 1)):
-            acc = score(fp4_cols(shelves_w, c0, width), shelves_plane, c0, width, bank)
-            nc.vector.tensor_tensor(dd[:, c0 : c0 + width], acc[:], f2[:, c0 : c0 + width], ALU.subtract)
+        nc.gpsimd.tensor_tensor(dd[:, D_SPLIT:], ends_sb[:, B_REST:], f2[:, D_SPLIT:], ALU.subtract)
+        for first, width, bank in ((0, BANK, 0), (BANK, D_SPLIT - BANK, 1)):
+            cols = slice(first, first + width)
+            acc = bank_tile(bank, width)
+            score_fp4(acc, 0, shelves_w, shelves_plane, first, (width,))
+            nc.vector.tensor_tensor(dd[:, cols], acc[:], f2[:, cols], ALU.subtract)
+
         dd_lo = sb.tile([P, HALF_SLOTS], F32, name="dd_lo")
         dd_hi = sb.tile([P, HALF_SLOTS], F32, name="dd_hi")
         nc.vector.tensor_copy(dd_lo[:], dd[:].indirect(idx6[:, :HALF_LIST]))
         nc.scalar.activation(dd_hi[:], dd[:].indirect(idx6[:, HALF_LIST:]), COPY)
-        for j, picked in ((1, dd_hi), (0, dd_lo)):
-            cols = slice(j * HALF_SLOTS, (j + 1) * HALF_SLOTS)
-            y = sb.tile([P, HALF_SLOTS], F32, name="y%d" % j)
-            nc.vector.tensor_tensor(y[:], picked[:], bb_pick[:, cols], ALU.max)
-            nc.sync.dma_start(out[:, cols], y[:])
+        for half, picked in ((1, dd_hi), (0, dd_lo)):
+            slots = slice(half * HALF_SLOTS, (half + 1) * HALF_SLOTS)
+            larger = sb.tile([P, HALF_SLOTS], F32, name="larger%d" % half)
+            nc.vector.tensor_tensor(larger[:], picked[:], bb_pick[:, slots], ALU.max)
+            nc.sync.dma_start(out[:, slots], larger[:])

from contextlib import ExitStack

import concourse.mybir as mybir

FEATURES, COLS, SLOTS, ROWS = 512, 1024, 512, 128
FLOPS = 2 * FEATURES * ROWS * 4 * COLS

F32 = mybir.dt.float32
BF16 = mybir.dt.bfloat16
I32 = mybir.dt.int32
U32 = mybir.dt.uint32
U16 = mybir.dt.uint16
U8 = mybir.dt.uint8
FP8X4 = mybir.dt.float8_e4m3fn_x4
FP4X4 = mybir.dt.float4_e2m1fn_x4
COPY = mybir.ActivationFunctionType.Copy
ALU = mybir.AluOpType

P = 128
PACK = 4
BANK = 512
HALF_SLOTS = SLOTS // 2
LIST_COLS = SLOTS // 16
HALF_LIST = LIST_COLS // 2

CAST_ON_VECTOR = 80
A_WIDTHS = (256, 256, 256, 128, 128)
A_ON_VECTOR = (0, 2)
D_SPLIT = 640
B_REST = BANK - (COLS - D_SPLIT)
B_SPLIT = COLS - B_REST


def tile_attend_twomarkets_four_kernel(
    tc, query, keys_words, keys_scales, notes_words, notes_scales, users_words, users_scales,
    shelves_words, shelves_scales, offs, offs2, offs3, offs4, offs5, offs6, out,
):
    nc = tc.nc
    with ExitStack() as ctx:
        lists = ctx.enter_context(tc.tile_pool(name="lists", bufs=1))
        sb = ctx.enter_context(tc.tile_pool(name="sb", bufs=1))
        psum = ctx.enter_context(tc.psum_pool(name="psum", bufs=1))

        def load_list(source, name):
            tile = lists.tile([P, LIST_COLS], U16, name=name)
            nc.sync.dma_start(tile[:], source)
            return tile

        def zeroed_plane(name):
            plane = sb.tile([P, COLS], U8, name=name, align_bytes=64)
            nc.vector.memset(plane[:].bitcast(I32), 0)
            return plane

        def load_scales(plane, scales):
            for quad in (0, 2, 1, 3):
                nc.sync.dma_start(
                    plane[32 * quad : 32 * quad + 4, :].bitcast(I32),
                    scales[0, 4 * quad : 4 * quad + 4, :].bitcast(I32),
                )

        def load_fp8_words(words, first, width, name):
            tile = sb.tile([P, width], U32, name=name, align_bytes=64)
            rows = words[0].rearrange("p n t -> p (n t)").bitcast(I32)
            nc.sync.dma_start(tile[:].bitcast(I32), rows[:, first : first + width])
            return tile

        def load_fp4_words(words, name):
            tile = sb.tile([P, 2 * COLS], U8, name=name, align_bytes=64)
            nc.sync.dma_start(tile[:].bitcast(I32), words[0].bitcast(I32))
            return tile

        keys_plane = zeroed_plane("keys_plane")
        q_raw = sb.tile([P, PACK, ROWS], F32, name="q_raw", align_bytes=64)
        nc.sync.dma_start(q_raw[:], query.rearrange("(p t) w -> p t w", t=PACK))
        keys_lo = load_fp8_words(keys_words, 0, BANK, "keys_lo")
        load_scales(keys_plane, keys_scales)
        keys_hi = load_fp8_words(keys_words, BANK, BANK, "keys_hi")
        idx = load_list(offs, "idx")

        users_plane = zeroed_plane("users_plane")
        notes_plane = zeroed_plane("notes_plane")
        shelves_plane = zeroed_plane("shelves_plane")
        f1 = sb.tile([P, COLS], F32, name="f1")
        nc.vector.memset(f1[:], 0.0)

        q_bf = sb.tile([P, ROWS, PACK], BF16, name="q_bf", tag="q_bf_then_f2", align_bytes=64)
        nc.vector.tensor_copy(
            out=q_bf[:, :CAST_ON_VECTOR, :].rearrange("p (c i) t -> p c t i", i=4),
            in_=q_raw[:, :, :CAST_ON_VECTOR].rearrange("p t (c i) -> p c t i", i=4),
        )
        nc.scalar.copy(
            out=q_bf[:, CAST_ON_VECTOR:, :].rearrange("p (c i) t -> p c t i", i=4),
            in_=q_raw[:, :, CAST_ON_VECTOR:].rearrange("p t (c i) -> p c t i", i=4),
        )
        q_codes = sb.tile([P, ROWS], U32, name="q_codes", align_bytes=64)
        q_plane = sb.tile([P, ROWS], U8, name="q_plane", align_bytes=64)
        nc.vector.quantize_mx(
            out=q_codes[:].bitcast(FP8X4), scales=q_plane[:], in_=q_bf[:].rearrange("p w t -> p (w t)")
        )
        f2 = sb.tile([P, COLS], F32, name="f2", tag="q_bf_then_f2", align_bytes=64)
        nc.vector.memset(f2[:], 0.0)

        users_w = load_fp8_words(users_words, 0, COLS, "users_w")
        load_scales(users_plane, users_scales)
        idx2 = load_list(offs2, "idx2")
        idx3 = load_list(offs3, "idx3")
        idx4 = load_list(offs4, "idx4")
        notes_w = load_fp4_words(notes_words, "notes_w")
        load_scales(notes_plane, notes_scales)
        shelves_w = load_fp4_words(shelves_words, "shelves_w")
        load_scales(shelves_plane, shelves_scales)
        idx5 = load_list(offs5, "idx5")
        idx6 = load_list(offs6, "idx6")

        def bank_tile(bank, width):
            return psum.tile([P, width], F32, name="acc", tag="bank%d" % bank)

        def score(acc, moving, moving_scale):
            nc.tensor.matmul_mx(
                out=acc, lhsT=q_codes[:].bitcast(FP8X4), lhsT_scale=q_plane[:],
                rhs=moving, rhs_scale=moving_scale, start=True, stop=True,
            )

        def score_fp4(acc, at, words, plane, first, widths):
            for width in widths:
                moving = words[:, 2 * first : 2 * (first + width)].bitcast(FP4X4)
                score(acc[:, at : at + width], moving, plane[:, first : first + width])
                at += width
                first += width

        a_sb = sb.tile([P, COLS], F32, name="a_sb")
        first = 0
        for piece, width in enumerate(A_WIDTHS):
            cols = slice(first, first + width)
            keys_half = (keys_lo, keys_hi)[first // BANK]
            acc = bank_tile(piece, width)
            score(acc[:], keys_half[:, first % BANK : first % BANK + width].bitcast(FP8X4), keys_plane[:, cols])
            if piece in A_ON_VECTOR:
                nc.vector.tensor_copy(a_sb[:, cols], acc[:])
            else:
                nc.scalar.copy(a_sb[:, cols], acc[:])
            first += width
        a_pick = sb.tile([P, SLOTS], F32, name="a_pick")
        nc.vector.tensor_copy(a_pick[:, :HALF_SLOTS], a_sb[:].indirect(idx[:, :HALF_LIST]))
        nc.scalar.activation(a_pick[:, HALF_SLOTS:], a_sb[:].indirect(idx[:, HALF_LIST:]), COPY)
        nc.vector.tensor_copy(f1[:].indirect(idx2[:]), a_pick[:])

        c_sb = sb.tile([P, COLS], F32, name="c_sb")
        for half in range(2):
            cols = slice(half * BANK, (half + 1) * BANK)
            acc = bank_tile(5 + half, BANK)
            score(acc[:], users_w[:, cols].bitcast(FP8X4), users_plane[:, cols])
            nc.scalar.copy(c_sb[:, cols], acc[:])
        c_pick = sb.tile([P, SLOTS], F32, name="c_pick")
        nc.scalar.activation(c_pick[:], c_sb[:].indirect(idx3[:]), COPY)
        nc.vector.tensor_copy(f2[:].indirect(idx4[:]), c_pick[:])

        b_sb = sb.tile([P, B_SPLIT], F32, name="b_sb")
        bb = sb.tile([P, COLS], F32, name="bb")
        for first, widths, bank in ((0, (BANK,), 7), (BANK, (256, 128), 3)):
            cols = slice(first, first + sum(widths))
            acc = bank_tile(bank, sum(widths))
            score_fp4(acc, 0, notes_w, notes_plane, first, widths)
            nc.scalar.copy(b_sb[:, cols], acc[:])
            nc.gpsimd.tensor_tensor(bb[:, cols], b_sb[:, cols], f1[:, cols], ALU.add)
        ends = bank_tile(2, BANK)
        score_fp4(ends, 0, notes_w, notes_plane, B_SPLIT, (B_REST,))
        score_fp4(ends, B_REST, shelves_w, shelves_plane, D_SPLIT, (256, 128))
        ends_sb = sb.tile([P, BANK], F32, name="ends_sb")
        nc.scalar.copy(ends_sb[:], ends[:])
        nc.gpsimd.tensor_tensor(bb[:, B_SPLIT:], ends_sb[:, :B_REST], f1[:, B_SPLIT:], ALU.add)
        bb_pick = sb.tile([P, SLOTS], F32, name="bb_pick")
        nc.scalar.activation(bb_pick[:], bb[:].indirect(idx5[:]), COPY)

        dd = sb.tile([P, COLS], F32, name="dd")
        nc.gpsimd.tensor_tensor(dd[:, D_SPLIT:], ends_sb[:, B_REST:], f2[:, D_SPLIT:], ALU.subtract)
        for first, width, bank in ((0, BANK, 0), (BANK, D_SPLIT - BANK, 1)):
            cols = slice(first, first + width)
            acc = bank_tile(bank, width)
            score_fp4(acc, 0, shelves_w, shelves_plane, first, (width,))
            nc.vector.tensor_tensor(dd[:, cols], acc[:], f2[:, cols], ALU.subtract)

        dd_lo = sb.tile([P, HALF_SLOTS], F32, name="dd_lo")
        dd_hi = sb.tile([P, HALF_SLOTS], F32, name="dd_hi")
        nc.vector.tensor_copy(dd_lo[:], dd[:].indirect(idx6[:, :HALF_LIST]))
        nc.scalar.activation(dd_hi[:], dd[:].indirect(idx6[:, HALF_LIST:]), COPY)
        for half, picked in ((1, dd_hi), (0, dd_lo)):
            slots = slice(half * HALF_SLOTS, (half + 1) * HALF_SLOTS)
            larger = sb.tile([P, HALF_SLOTS], F32, name="larger%d" % half)
            nc.vector.tensor_tensor(larger[:], picked[:], bb_pick[:, slots], ALU.max)
            nc.sync.dma_start(out[:, slots], larger[:])
